import numpy as np
import ml_dtypes


def mxq(x, axis, fmt="e4m3"):
    dtype, down = {"e4m3": (ml_dtypes.float8_e4m3fn, 7), "e5m2": (ml_dtypes.float8_e5m2, 14)}[fmt]
    v = np.moveaxis(np.asarray(x, np.float32).astype(ml_dtypes.bfloat16).astype(np.float64), axis, -1)
    blocks = v.reshape(v.shape[:-1] + (-1, 32))
    amax = np.abs(blocks).max(-1, keepdims=True)
    byte = np.maximum(np.where(amax > 0, np.frexp(amax)[1] - 1 + 127, 0) - down, 1)
    scale = np.exp2(byte - 127.0)
    codes = (blocks / scale).astype(np.float32).astype(dtype).astype(np.float64)
    return np.moveaxis((codes * scale).reshape(v.shape), -1, axis)


WIDE = False


def mx_kscale(k):
    if not WIDE:
        return np.ones(k)
    levels = np.array([10, -10, 5, -5, 0])
    if k % 512:
        return np.exp2(np.random.permutation(np.resize(levels, k // 32))).repeat(32)
    a = np.empty((k // 512, 16))
    for p in range(k // 512):
        a[p, :8] = np.random.permutation(np.resize(levels, 8))
        for g in range(8):
            far = levels[np.abs(levels - a[p, g]) >= 10]
            a[p, g + 8] = far[np.random.randint(len(far))]
    return np.exp2(a.ravel()).repeat(32)


def f64(x):
    return np.asarray(x).astype(np.float64)


def striped(idx):
    return np.tile(idx.reshape(-1, 16).T, (8, 1)).astype(np.uint16)


def unstriped(offs):
    return offs[:16].T.reshape(-1).astype(np.int64)


def pack_weight(w):
    k, n = w.shape
    w = f64(np.asarray(w, np.float32).astype(ml_dtypes.bfloat16)).reshape(k // 32, 32, n)
    amax = np.abs(w).max(1)
    byte = np.clip(np.where(amax > 0, np.frexp(amax)[1] - 1 + 127 - 7, 1), 1, 254)
    scaled = (w * np.exp2(127.0 - byte)[:, None, :]).reshape(k, n).astype(np.float32)
    words = np.ascontiguousarray(scaled.reshape(k // 512, 128, 4, n).transpose(0, 1, 3, 2)).astype(ml_dtypes.float8_e4m3fn).view(np.uint8)
    return words, np.ascontiguousarray(byte.astype(np.uint8).reshape(k // 512, 16, n))


def unpack_weight(words, scales):
    g, p, n, _ = words.shape
    vals = np.ascontiguousarray(words).view(ml_dtypes.float8_e4m3fn).astype(np.float64) * np.repeat(np.exp2(scales.astype(np.float64) - 127.0), 8, axis=1)[..., None]
    return vals.transpose(0, 1, 3, 2).reshape(g * 512, n)


def relu(v):
    return np.maximum(v, 0.0)


K, T, S, N = 512, 1024, 512, 256


def setup_inputs():
    n = np.random.standard_normal
    s = mx_kscale(K)[:, None]
    packed_xT = pack_weight(n((K, T)) * s)
    return {
        "x_words": packed_xT[0],
        "x_scales": packed_xT[1],
        "w1": (n((K, N)) / np.sqrt(K) / s).astype(np.float32),
        "w2": (n((K, N)) / np.sqrt(K) / s).astype(np.float32),
        "head": (np.random.uniform(0.4, 1.2, (N, 1))).astype(np.float32),
        "inv0": (np.random.uniform(0.4, 0.8, (N, 1))).astype(np.float32),
        "offs": striped(np.random.permutation(T)[:S]),
        "lead": striped(np.random.permutation(S)),
        "alt": striped(np.random.permutation(S)),
    }


def reference(x_words, x_scales, w1, w2, head, inv0, offs, lead, alt):
    xq = unpack_weight(x_words, x_scales)[:, unstriped(offs)]
    y = mxq(f64(w1), 0, "e4m3").T @ xq
    spd = np.log(np.exp(y) + 1.0)
    dv = spd - spd[:, unstriped(lead)]
    ss = relu(f64(head) * spd + 0.5 * (spd * dv)) + 0.3
    z = mxq(f64(w2), 0, "e4m3").T @ xq
    gap = np.log(np.exp(z) + 1.0) + 0.5
    ac = -1.0 * (((f64(inv0) * spd) ** 2) ** 2) + 1.0 - ((ss / gap) ** 2)
    return ac[:, unstriped(alt)] - ac + 0.2 * ac[:, unstriped(lead)]

@@ -1,0 +1,165 @@
+import math
+from contextlib import ExitStack
+
+import concourse.mybir as mybir
+
+K, T, S, N = 512, 1024, 512, 256
+FLOPS = 2 * 2 * K * N * S
+
+F32 = mybir.dt.float32
+BF16 = mybir.dt.bfloat16
+I32 = mybir.dt.int32
+U32 = mybir.dt.uint32
+U16 = mybir.dt.uint16
+U8 = mybir.dt.uint8
+FP8X4 = mybir.dt.float8_e4m3fn_x4
+ALU = mybir.AluOpType
+ACT = mybir.ActivationFunctionType
+
+P = 128
+PACK = 4
+BLOCKS = N // P
+EXP_CAP = 2.0**60
+ROOT_E = math.exp(0.5)
+
+
+def tile_picked_yidm_mobil_p_kernel(
+    tc, x_words, x_scales, w1, w2, head, inv0, offs, lead, alt, out
+):
+    nc = tc.nc
+    with ExitStack() as ctx:
+        pool = ctx.enter_context(tc.tile_pool(name="pool", bufs=1))
+        psum = ctx.enter_context(tc.psum_pool(name="psum", bufs=1))
+
+        offs_t = pool.tile([P, S // 16], U16, name="offs_t")
+        lead_t = pool.tile([P, S // 16], U16, name="lead_t")
+        alt_t = pool.tile([P, S // 16], U16, name="alt_t")
+        words = pool.tile([P, T], I32, name="words", align_bytes=64)
+        scales = pool.tile([P, T], U8, name="scales", align_bytes=64)
+        raw = [pool.tile([P, PACK, N], F32, name="raw%d" % i) for i in range(2)]
+        head_t = pool.tile([P, BLOCKS], F32, name="head_t")
+        inv_t = pool.tile([P, BLOCKS], F32, name="inv_t")
+
+        nc.vector.memset(scales[:].bitcast(I32), 0)
+        nc.sync.dma_start(offs_t[:], offs)
+        for q in range(4):
+            nc.sync.dma_start(
+                scales[32 * q : 32 * q + 4, :].bitcast(I32),
+                x_scales[0, 4 * q : 4 * q + 4, :].bitcast(I32),
+            )
+        nc.sync.dma_start(words[:], x_words[0].rearrange("p n t -> p (n t)").bitcast(I32))
+        for i, w in enumerate((w1, w2)):
+            nc.sync.dma_start(raw[i][:], w.rearrange("(p j) m -> p j m", j=PACK))
+        nc.sync.dma_start(lead_t[:], lead)
+        nc.sync.dma_start(alt_t[:], alt)
+        with nc.allow_non_contiguous_dma(reason="one value a row"):
+            nc.sync.dma_start(head_t[:], head.rearrange("(b p) o -> p (b o)", p=P))
+            nc.sync.dma_start(inv_t[:], inv0.rearrange("(b p) o -> p (b o)", p=P))
+
+        x_codes = pool.tile([P, S], U32, name="x_codes", align_bytes=64)
+        x_plane = pool.tile([P, S], U8, name="x_plane", align_bytes=64)
+        nc.vector.tensor_copy(x_plane[:], scales[:].indirect(offs_t[:]))
+        nc.vector.tensor_copy(x_codes[:], words[:].bitcast(U32).indirect(offs_t[:]))
+
+        acc = {}
+        expd = pool.tile([P, 2 * BLOCKS * S], F32, name="expd")
+        capped = pool.tile([P, 2 * BLOCKS * S], F32, name="capped")
+        for i in range(2):
+            grouped = pool.tile([P, N * PACK], BF16, name="grouped%d" % i, align_bytes=64)
+            codes = pool.tile([P, N], U32, name="codes%d" % i, align_bytes=64)
+            plane = pool.tile([P, N], U8, name="plane%d" % i, align_bytes=64)
+            for b in range(BLOCKS):
+                dst = grouped[:, b * P * PACK : (b + 1) * P * PACK].rearrange("p (c i t) -> p c t i", i=4, t=PACK)
+                src = raw[i][:, :, b * P : (b + 1) * P].rearrange("p t (c i) -> p c t i", i=4)
+                if i == 0:
+                    nc.scalar.copy(dst, src)
+                else:
+                    nc.vector.tensor_copy(dst, src)
+            for b in range(BLOCKS):
+                m = slice(b * P, (b + 1) * P)
+                nc.vector.quantize_mx(
+                    out=codes[:, m].bitcast(FP8X4), scales=plane[:, m], in_=grouped[:, b * P * PACK : (b + 1) * P * PACK]
+                )
+                acc[i, b] = psum.tile([P, S], F32, name="acc%d%d" % (i, b))
+                nc.tensor.matmul_mx(
+                    out=acc[i, b][:],
+                    lhsT=codes[:, m].bitcast(FP8X4),
+                    lhsT_scale=plane[:, m],
+                    rhs=x_codes[:].bitcast(FP8X4),
+                    rhs_scale=x_plane[:],
+                    start=True,
+                    stop=True,
+                )
+                c0 = (i * BLOCKS + b) * S
+                nc.scalar.activation(expd[:, c0 : c0 + S], acc[i, b][:], ACT.Exp)
+
+        nc.vector.tensor_scalar(capped[:], expd[:], EXP_CAP, None, ALU.min)
+
+        lo, hi = slice(0, S), slice(S, 2 * S)
+        spd_w = [pool.tile([P, 2 * S], F32, name="spd_w%d" % b) for b in range(BLOCKS)]
+        neg_w = [pool.tile([P, 2 * S], F32, name="neg_w%d" % b) for b in range(BLOCKS)]
+        fifth_w = [pool.tile([P, 2 * S], F32, name="fifth_w%d" % b) for b in range(BLOCKS)]
+        soft_z = pool.tile([P, BLOCKS * S], F32, name="soft_z")
+        gap = pool.tile([P, BLOCKS * S], F32, name="gap")
+        log_gap = pool.tile([P, BLOCKS * S], F32, name="log_gap")
+
+        for b in range(BLOCKS):
+            cols = slice(b * S, (b + 1) * S)
+            c0 = (BLOCKS + b) * S
+            nc.scalar.activation(soft_z[:, cols], capped[:, c0 : c0 + S], ACT.Ln, bias=ROOT_E, scale=ROOT_E)
+            nc.vector.scalar_tensor_tensor(gap[:, cols], acc[1, b][:], 0.5, soft_z[:, cols], ALU.add, ALU.max)
+        for b in range(BLOCKS):
+            cols = slice(b * S, (b + 1) * S)
+            nc.scalar.activation(spd_w[b][:, hi], capped[:, cols], ACT.Ln, bias=1.0)
+            nc.vector.tensor_tensor(spd_w[b][:, lo], acc[0, b][:], spd_w[b][:, hi], ALU.max)
+        nc.scalar.activation(log_gap[:], gap[:], ACT.Ln, scale=2.0)
+
+        shifted = [pool.tile([P, S], F32, name="shifted%d" % b) for b in range(BLOCKS)]
+        diff = [pool.tile([P, S], F32, name="diff%d" % b) for b in range(BLOCKS)]
+        wish = [pool.tile([P, S], F32, name="wish%d" % b) for b in range(BLOCKS)]
+        recip = [pool.tile([P, S], F32, name="recip%d" % b) for b in range(BLOCKS)]
+        for b in range(BLOCKS):
+            h = head_t[:, b : b + 1]
+            nc.vector.tensor_scalar(shifted[b][:], spd_w[b][:, lo], h, h, ALU.add, ALU.add)
+        for b in range(BLOCKS):
+            nc.vector.tensor_tensor(diff[b][:], spd_w[b][:].indirect(lead_t[:]), shifted[b][:], ALU.subtract)
+        for b in range(BLOCKS):
+            nc.vector.scalar_tensor_tensor(wish[b][:], diff[b][:], 0.0, spd_w[b][:, lo], ALU.min, ALU.mult)
+        for b in range(BLOCKS):
+            nc.scalar.activation(recip[b][:], log_gap[:, b * S : (b + 1) * S], ACT.Exp, scale=-1.0)
+            nc.vector.scalar_tensor_tensor(neg_w[b][:, hi], wish[b][:], -0.6, recip[b][:], ALU.add, ALU.mult)
+
+        fourth = [pool.tile([P, S], F32, name="fourth%d" % b) for b in range(BLOCKS)]
+        ratio2 = [pool.tile([P, S], F32, name="ratio2%d" % b) for b in range(BLOCKS)]
+        part = [pool.tile([P, S], F32, name="part%d" % b) for b in range(BLOCKS)]
+        res = [fourth[1], pool.tile([P, S], F32, name="res1")]
+
+        def fourth_power(b):
+            nc.scalar.activation(fifth_w[b][:, hi], spd_w[b][:, lo], ACT.Square, scale=inv_t[:, b : b + 1])
+            nc.scalar.activation(fourth[b][:], fifth_w[b][:, hi], ACT.Square)
+
+        def negated(b):
+            nc.vector.scalar_tensor_tensor(neg_w[b][:, lo], ratio2[b][:], -1.0, fourth[b][:], ALU.mult, ALU.subtract)
+
+        def by_lead(b):
+            nc.vector.tensor_tensor(part[b][:], fifth_w[b][:].indirect(lead_t[:]), neg_w[b][:, lo], ALU.subtract)
+
+        def by_alt(b, c0, c1):
+            nc.vector.tensor_tensor(
+                res[b][:, c0:c1], neg_w[b][:].indirect(alt_t[:, c0 // 16 : c1 // 16]), part[b][:, c0:c1], ALU.add
+            )
+            nc.sync.dma_start(out[b * P : (b + 1) * P, c0:c1], res[b][:, c0:c1])
+
+        fourth_power(0)
+        for b in range(BLOCKS):
+            nc.scalar.activation(ratio2[b][:], neg_w[b][:, hi], ACT.Square)
+        fourth_power(1)
+        negated(0)
+        nc.vector.tensor_scalar(fifth_w[0][:, lo], neg_w[0][:, lo], 0.2, 0.2, ALU.mult, ALU.add)
+        by_lead(0)
+        negated(1)
+        nc.scalar.activation(fifth_w[1][:, lo], neg_w[1][:, lo], ACT.Copy, bias=0.2, scale=0.2)
+        by_alt(0, 0, S)
+        by_lead(1)
+        by_alt(1, 0, 384)
+        by_alt(1, 384, S)

@@ -64,8 +64,8 @@ def tile_picked_yidm_mobil_p_kernel(
         acc = {}
         expd = pool.tile([P, 2 * BLOCKS * S], F32, name="expd")
         capped = pool.tile([P, 2 * BLOCKS * S], F32, name="capped")
+        grouped = pool.tile([P, N * PACK], BF16, name="grouped", align_bytes=64)
         for i in range(2):
-            grouped = pool.tile([P, N * PACK], BF16, name="grouped%d" % i, align_bytes=64)
             codes = pool.tile([P, N], U32, name="codes%d" % i, align_bytes=64)
             plane = pool.tile([P, N], U8, name="plane%d" % i, align_bytes=64)
             for b in range(BLOCKS):
@@ -102,47 +102,61 @@ def tile_picked_yidm_mobil_p_kernel(
         soft_z = pool.tile([P, BLOCKS * S], F32, name="soft_z")
         gap = pool.tile([P, BLOCKS * S], F32, name="gap")
         log_gap = pool.tile([P, BLOCKS * S], F32, name="log_gap")
+        shifted = [pool.tile([P, S], F32, name="shifted%d" % b) for b in range(BLOCKS)]
+        diff = [pool.tile([P, S], F32, name="diff%d" % b) for b in range(BLOCKS)]
+        recip = [pool.tile([P, S], F32, name="recip%d" % b) for b in range(BLOCKS)]
+        square = [pool.tile([P, S], F32, name="square%d" % b) for b in range(BLOCKS)]
+        part = [pool.tile([P, S], F32, name="part%d" % b) for b in range(BLOCKS)]
+        wish0 = pool.tile([P, S], F32, name="wish0")
+        ratio = pool.tile([P, S], F32, name="ratio")
+        res1 = pool.tile([P, S], F32, name="res1")
+        wish = [wish0[:], log_gap[:, lo]]
+        res = [ratio, res1]
 
-        for b in range(BLOCKS):
+        def soft_gap(b):
             cols = slice(b * S, (b + 1) * S)
             c0 = (BLOCKS + b) * S
             nc.scalar.activation(soft_z[:, cols], capped[:, c0 : c0 + S], ACT.Ln, bias=ROOT_E, scale=ROOT_E)
             nc.vector.scalar_tensor_tensor(gap[:, cols], acc[1, b][:], 0.5, soft_z[:, cols], ALU.add, ALU.max)
-        for b in range(BLOCKS):
-            cols = slice(b * S, (b + 1) * S)
-            nc.scalar.activation(spd_w[b][:, hi], capped[:, cols], ACT.Ln, bias=1.0)
-            nc.vector.tensor_tensor(spd_w[b][:, lo], acc[0, b][:], spd_w[b][:, hi], ALU.max)
-        nc.scalar.activation(log_gap[:], gap[:], ACT.Ln, scale=2.0)
 
-        shifted = [pool.tile([P, S], F32, name="shifted%d" % b) for b in range(BLOCKS)]
-        diff = [pool.tile([P, S], F32, name="diff%d" % b) for b in range(BLOCKS)]
-        wish = [pool.tile([P, S], F32, name="wish%d" % b) for b in range(BLOCKS)]
-        recip = [pool.tile([P, S], F32, name="recip%d" % b) for b in range(BLOCKS)]
-        for b in range(BLOCKS):
+        def soft_speed(b):
+            nc.scalar.activation(spd_w[b][:, hi], capped[:, b * S : (b + 1) * S], ACT.Ln, bias=1.0)
+            nc.vector.tensor_tensor(spd_w[b][:, lo], acc[0, b][:], spd_w[b][:, hi], ALU.max)
+
+        def shift(b):
             h = head_t[:, b : b + 1]
             nc.vector.tensor_scalar(shifted[b][:], spd_w[b][:, lo], h, h, ALU.add, ALU.add)
-        for b in range(BLOCKS):
-            nc.vector.tensor_tensor(diff[b][:], spd_w[b][:].indirect(lead_t[:]), shifted[b][:], ALU.subtract)
-        for b in range(BLOCKS):
-            nc.vector.scalar_tensor_tensor(wish[b][:], diff[b][:], 0.0, spd_w[b][:, lo], ALU.min, ALU.mult)
-        for b in range(BLOCKS):
-            nc.scalar.activation(recip[b][:], log_gap[:, b * S : (b + 1) * S], ACT.Exp, scale=-1.0)
-            nc.vector.scalar_tensor_tensor(neg_w[b][:, hi], wish[b][:], -0.6, recip[b][:], ALU.add, ALU.mult)
 
-        fourth = [pool.tile([P, S], F32, name="fourth%d" % b) for b in range(BLOCKS)]
-        ratio2 = [pool.tile([P, S], F32, name="ratio2%d" % b) for b in range(BLOCKS)]
-        part = [pool.tile([P, S], F32, name="part%d" % b) for b in range(BLOCKS)]
-        res = [fourth[1], pool.tile([P, S], F32, name="res1")]
+        def leader(b):
+            nc.vector.tensor_tensor(diff[b][:], spd_w[b][:].indirect(lead_t[:]), shifted[b][:], ALU.subtract)
+
+        def wished(b):
+            nc.vector.scalar_tensor_tensor(wish[b], diff[b][:], 0.0, spd_w[b][:, lo], ALU.min, ALU.mult)
+
+        def inverse_gap(b):
+            nc.scalar.activation(recip[b][:], log_gap[:, b * S : (b + 1) * S], ACT.Exp, scale=-1.0)
+
+        def quotient(b):
+            nc.vector.scalar_tensor_tensor(ratio[:], wish[b], -0.6, recip[b][:], ALU.add, ALU.mult)
+            nc.scalar.activation(neg_w[b][:, hi], ratio[:], ACT.Square)
 
         def fourth_power(b):
-            nc.scalar.activation(fifth_w[b][:, hi], spd_w[b][:, lo], ACT.Square, scale=inv_t[:, b : b + 1])
-            nc.scalar.activation(fourth[b][:], fifth_w[b][:, hi], ACT.Square)
+            nc.scalar.activation(square[b][:], spd_w[b][:, lo], ACT.Square, scale=inv_t[:, b : b + 1])
+            nc.scalar.activation(fifth_w[b][:, hi], square[b][:], ACT.Square)
 
         def negated(b):
-            nc.vector.scalar_tensor_tensor(neg_w[b][:, lo], ratio2[b][:], -1.0, fourth[b][:], ALU.mult, ALU.subtract)
+            nc.vector.scalar_tensor_tensor(
+                neg_w[b][:, lo], neg_w[b][:, hi], -1.0, fifth_w[b][:, hi], ALU.mult, ALU.subtract
+            )
+            nc.scalar.activation(fifth_w[b][:, lo], neg_w[b][:, lo], ACT.Copy, bias=0.2, scale=0.2)
 
-        def by_lead(b):
-            nc.vector.tensor_tensor(part[b][:], fifth_w[b][:].indirect(lead_t[:]), neg_w[b][:, lo], ALU.subtract)
+        def by_lead(b, c0, c1):
+            nc.vector.tensor_tensor(
+                part[b][:, c0:c1],
+                fifth_w[b][:].indirect(lead_t[:, c0 // 16 : c1 // 16]),
+                neg_w[b][:, c0:c1],
+                ALU.subtract,
+            )
 
         def by_alt(b, c0, c1):
             nc.vector.tensor_tensor(
@@ -150,16 +164,28 @@ def tile_picked_yidm_mobil_p_kernel(
             )
             nc.sync.dma_start(out[b * P : (b + 1) * P, c0:c1], res[b][:, c0:c1])
 
+        soft_gap(0)
+        soft_speed(0)
+        soft_gap(1)
+        shift(0)
+        soft_speed(1)
+        nc.scalar.activation(log_gap[:], gap[:], ACT.Ln, scale=2.0)
+        leader(0)
+        shift(1)
+        wished(0)
+        leader(1)
+        inverse_gap(0)
         fourth_power(0)
-        for b in range(BLOCKS):
-            nc.scalar.activation(ratio2[b][:], neg_w[b][:, hi], ACT.Square)
-        fourth_power(1)
+        inverse_gap(1)
+        quotient(0)
+        wished(1)
         negated(0)
-        nc.vector.tensor_scalar(fifth_w[0][:, lo], neg_w[0][:, lo], 0.2, 0.2, ALU.mult, ALU.add)
-        by_lead(0)
+        quotient(1)
+        fourth_power(1)
+        by_lead(0, 0, S)
         negated(1)
-        nc.scalar.activation(fifth_w[1][:, lo], neg_w[1][:, lo], ACT.Copy, bias=0.2, scale=0.2)
         by_alt(0, 0, S)
-        by_lead(1)
+        by_lead(1, 0, 384)
+        by_lead(1, 384, S)
         by_alt(1, 0, 384)
         by_alt(1, 384, S)

@@ -42,12 +42,12 @@ def tile_picked_yidm_mobil_p_kernel(
 
         nc.vector.memset(scales[:].bitcast(I32), 0)
         nc.sync.dma_start(offs_t[:], offs)
+        nc.sync.dma_start(words[:], x_words[0].rearrange("p n t -> p (n t)").bitcast(I32))
         for q in range(4):
             nc.sync.dma_start(
                 scales[32 * q : 32 * q + 4, :].bitcast(I32),
                 x_scales[0, 4 * q : 4 * q + 4, :].bitcast(I32),
             )
-        nc.sync.dma_start(words[:], x_words[0].rearrange("p n t -> p (n t)").bitcast(I32))
         for i, w in enumerate((w1, w2)):
             nc.sync.dma_start(raw[i][:], w.rearrange("(p j) m -> p j m", j=PACK))
         nc.sync.dma_start(lead_t[:], lead)
@@ -58,8 +58,8 @@ def tile_picked_yidm_mobil_p_kernel(
 
         x_codes = pool.tile([P, S], U32, name="x_codes", align_bytes=64)
         x_plane = pool.tile([P, S], U8, name="x_plane", align_bytes=64)
-        nc.vector.tensor_copy(x_plane[:], scales[:].indirect(offs_t[:]))
         nc.vector.tensor_copy(x_codes[:], words[:].bitcast(U32).indirect(offs_t[:]))
+        nc.vector.tensor_copy(x_plane[:], scales[:].indirect(offs_t[:]))
 
         acc = {}
         expd = pool.tile([P, 2 * BLOCKS * S], F32, name="expd")

import math
from contextlib import ExitStack

import concourse.mybir as mybir

K, T, S, N = 512, 1024, 512, 256
FLOPS = 2 * 2 * K * N * S

F32 = mybir.dt.float32
BF16 = mybir.dt.bfloat16
I32 = mybir.dt.int32
U32 = mybir.dt.uint32
U16 = mybir.dt.uint16
U8 = mybir.dt.uint8
FP8X4 = mybir.dt.float8_e4m3fn_x4
ALU = mybir.AluOpType
ACT = mybir.ActivationFunctionType

P = 128
PACK = 4
BLOCKS = N // P
EXP_CAP = 2.0**60
ROOT_E = math.exp(0.5)


def tile_picked_yidm_mobil_p_kernel(
    tc, x_words, x_scales, w1, w2, head, inv0, offs, lead, alt, out
):
    nc = tc.nc
    with ExitStack() as ctx:
        pool = ctx.enter_context(tc.tile_pool(name="pool", bufs=1))
        psum = ctx.enter_context(tc.psum_pool(name="psum", bufs=1))

        offs_t = pool.tile([P, S // 16], U16, name="offs_t")
        lead_t = pool.tile([P, S // 16], U16, name="lead_t")
        alt_t = pool.tile([P, S // 16], U16, name="alt_t")
        words = pool.tile([P, T], I32, name="words", align_bytes=64)
        scales = pool.tile([P, T], U8, name="scales", align_bytes=64)
        raw = [pool.tile([P, PACK, N], F32, name="raw%d" % i) for i in range(2)]
        head_t = pool.tile([P, BLOCKS], F32, name="head_t")
        inv_t = pool.tile([P, BLOCKS], F32, name="inv_t")

        nc.vector.memset(scales[:].bitcast(I32), 0)
        nc.sync.dma_start(offs_t[:], offs)
        nc.sync.dma_start(words[:], x_words[0].rearrange("p n t -> p (n t)").bitcast(I32))
        for q in range(4):
            nc.sync.dma_start(
                scales[32 * q : 32 * q + 4, :].bitcast(I32),
                x_scales[0, 4 * q : 4 * q + 4, :].bitcast(I32),
            )
        for i, w in enumerate((w1, w2)):
            nc.sync.dma_start(raw[i][:], w.rearrange("(p j) m -> p j m", j=PACK))
        nc.sync.dma_start(lead_t[:], lead)
        nc.sync.dma_start(alt_t[:], alt)
        with nc.allow_non_contiguous_dma(reason="one value a row"):
            nc.sync.dma_start(head_t[:], head.rearrange("(b p) o -> p (b o)", p=P))
            nc.sync.dma_start(inv_t[:], inv0.rearrange("(b p) o -> p (b o)", p=P))

        x_codes = pool.tile([P, S], U32, name="x_codes", align_bytes=64)
        x_plane = pool.tile([P, S], U8, name="x_plane", align_bytes=64)
        nc.vector.tensor_copy(x_codes[:], words[:].bitcast(U32).indirect(offs_t[:]))
        nc.vector.tensor_copy(x_plane[:], scales[:].indirect(offs_t[:]))

        acc = {}
        expd = pool.tile([P, 2 * BLOCKS * S], F32, name="expd")
        capped = pool.tile([P, 2 * BLOCKS * S], F32, name="capped")
        grouped = pool.tile([P, N * PACK], BF16, name="grouped", align_bytes=64)
        for i in range(2):
            codes = pool.tile([P, N], U32, name="codes%d" % i, align_bytes=64)
            plane = pool.tile([P, N], U8, name="plane%d" % i, align_bytes=64)
            for b in range(BLOCKS):
                dst = grouped[:, b * P * PACK : (b + 1) * P * PACK].rearrange("p (c i t) -> p c t i", i=4, t=PACK)
                src = raw[i][:, :, b * P : (b + 1) * P].rearrange("p t (c i) -> p c t i", i=4)
                if i == 0:
                    nc.scalar.copy(dst, src)
                else:
                    nc.vector.tensor_copy(dst, src)
            for b in range(BLOCKS):
                m = slice(b * P, (b + 1) * P)
                nc.vector.quantize_mx(
                    out=codes[:, m].bitcast(FP8X4), scales=plane[:, m], in_=grouped[:, b * P * PACK : (b + 1) * P * PACK]
                )
                acc[i, b] = psum.tile([P, S], F32, name="acc%d%d" % (i, b))
                nc.tensor.matmul_mx(
                    out=acc[i, b][:],
                    lhsT=codes[:, m].bitcast(FP8X4),
                    lhsT_scale=plane[:, m],
                    rhs=x_codes[:].bitcast(FP8X4),
                    rhs_scale=x_plane[:],
                    start=True,
                    stop=True,
                )
                c0 = (i * BLOCKS + b) * S
                nc.scalar.activation(expd[:, c0 : c0 + S], acc[i, b][:], ACT.Exp)

        nc.vector.tensor_scalar(capped[:], expd[:], EXP_CAP, None, ALU.min)

        lo, hi = slice(0, S), slice(S, 2 * S)
        spd_w = [pool.tile([P, 2 * S], F32, name="spd_w%d" % b) for b in range(BLOCKS)]
        neg_w = [pool.tile([P, 2 * S], F32, name="neg_w%d" % b) for b in range(BLOCKS)]
        fifth_w = [pool.tile([P, 2 * S], F32, name="fifth_w%d" % b) for b in range(BLOCKS)]
        soft_z = pool.tile([P, BLOCKS * S], F32, name="soft_z")
        gap = pool.tile([P, BLOCKS * S], F32, name="gap")
        log_gap = pool.tile([P, BLOCKS * S], F32, name="log_gap")
        shifted = [pool.tile([P, S], F32, name="shifted%d" % b) for b in range(BLOCKS)]
        diff = [pool.tile([P, S], F32, name="diff%d" % b) for b in range(BLOCKS)]
        recip = [pool.tile([P, S], F32, name="recip%d" % b) for b in range(BLOCKS)]
        square = [pool.tile([P, S], F32, name="square%d" % b) for b in range(BLOCKS)]
        part = [pool.tile([P, S], F32, name="part%d" % b) for b in range(BLOCKS)]
        wish0 = pool.tile([P, S], F32, name="wish0")
        ratio = pool.tile([P, S], F32, name="ratio")
        res1 = pool.tile([P, S], F32, name="res1")
        wish = [wish0[:], log_gap[:, lo]]
        res = [ratio, res1]

        def soft_gap(b):
            cols = slice(b * S, (b + 1) * S)
            c0 = (BLOCKS + b) * S
            nc.scalar.activation(soft_z[:, cols], capped[:, c0 : c0 + S], ACT.Ln, bias=ROOT_E, scale=ROOT_E)
            nc.vector.scalar_tensor_tensor(gap[:, cols], acc[1, b][:], 0.5, soft_z[:, cols], ALU.add, ALU.max)

        def soft_speed(b):
            nc.scalar.activation(spd_w[b][:, hi], capped[:, b * S : (b + 1) * S], ACT.Ln, bias=1.0)
            nc.vector.tensor_tensor(spd_w[b][:, lo], acc[0, b][:], spd_w[b][:, hi], ALU.max)

        def shift(b):
            h = head_t[:, b : b + 1]
            nc.vector.tensor_scalar(shifted[b][:], spd_w[b][:, lo], h, h, ALU.add, ALU.add)

        def leader(b):
            nc.vector.tensor_tensor(diff[b][:], spd_w[b][:].indirect(lead_t[:]), shifted[b][:], ALU.subtract)

        def wished(b):
            nc.vector.scalar_tensor_tensor(wish[b], diff[b][:], 0.0, spd_w[b][:, lo], ALU.min, ALU.mult)

        def inverse_gap(b):
            nc.scalar.activation(recip[b][:], log_gap[:, b * S : (b + 1) * S], ACT.Exp, scale=-1.0)

        def quotient(b):
            nc.vector.scalar_tensor_tensor(ratio[:], wish[b], -0.6, recip[b][:], ALU.add, ALU.mult)
            nc.scalar.activation(neg_w[b][:, hi], ratio[:], ACT.Square)

        def fourth_power(b):
            nc.scalar.activation(square[b][:], spd_w[b][:, lo], ACT.Square, scale=inv_t[:, b : b + 1])
            nc.scalar.activation(fifth_w[b][:, hi], square[b][:], ACT.Square)

        def negated(b):
            nc.vector.scalar_tensor_tensor(
                neg_w[b][:, lo], neg_w[b][:, hi], -1.0, fifth_w[b][:, hi], ALU.mult, ALU.subtract
            )
            nc.scalar.activation(fifth_w[b][:, lo], neg_w[b][:, lo], ACT.Copy, bias=0.2, scale=0.2)

        def by_lead(b, c0, c1):
            nc.vector.tensor_tensor(
                part[b][:, c0:c1],
                fifth_w[b][:].indirect(lead_t[:, c0 // 16 : c1 // 16]),
                neg_w[b][:, c0:c1],
                ALU.subtract,
            )

        def by_alt(b, c0, c1):
            nc.vector.tensor_tensor(
                res[b][:, c0:c1], neg_w[b][:].indirect(alt_t[:, c0 // 16 : c1 // 16]), part[b][:, c0:c1], ALU.add
            )
            nc.sync.dma_start(out[b * P : (b + 1) * P, c0:c1], res[b][:, c0:c1])

        soft_gap(0)
        soft_speed(0)
        soft_gap(1)
        shift(0)
        soft_speed(1)
        nc.scalar.activation(log_gap[:], gap[:], ACT.Ln, scale=2.0)
        leader(0)
        shift(1)
        wished(0)
        leader(1)
        inverse_gap(0)
        fourth_power(0)
        inverse_gap(1)
        quotient(0)
        wished(1)
        negated(0)
        quotient(1)
        fourth_power(1)
        by_lead(0, 0, S)
        negated(1)
        by_alt(0, 0, S)
        by_lead(1, 0, 384)
        by_lead(1, 384, S)
        by_alt(1, 0, 384)
        by_alt(1, 384, S)
